import numpy as np, ml_dtypes
CORES = [24,25,26,27,28,29,30,31]
N = 8
import mx_ref
BF = ml_dtypes.bfloat16
def gcols(t, e):
    v = np.concatenate([t.reshape(8, 16, -1, 4), np.zeros((8, 16, 1, 4), BF)], axis=2)
    return np.ascontiguousarray(np.stack([v[g][:, e[g]] for g in range(8)])).reshape(128, -1)
def tile(rs):
    return np.stack(rs, axis=2).reshape(128, -1).astype(BF)
def f(rng, *shape):
    return mx_ref.flush((rng.standard_normal(shape, dtype=np.float32) * np.exp2(rng.integers(-2, 3, shape[:-1] + (1,)))).astype(BF))
def wide(rng, *shape, cols=0):
    v = rng.standard_normal(shape, dtype=np.float32) * np.exp2(rng.integers(-12, 13, shape)).astype(np.float32)
    if cols: v *= np.repeat(np.exp2(rng.integers(-cols, cols + 1, shape[:-2] + (1, shape[-1] // 4))) * (rng.random(shape[:-2] + (1, shape[-1] // 4)) > 0.0625), 4, axis=-1).astype(np.float32)
    return mx_ref.flush(v.astype(BF))
T, SH = 256, 32
def shifts(s):
    return np.stack([np.repeat(s, 16, axis=0).astype(np.int32)] * N)
def setup_inputs(rng):
    return {"x": f(rng, N, 128, 4 * T), "w": np.stack([f(rng, 128, 6144)] * N), "v": f(rng, N, 128, 512), "sf": shifts(rng.integers(0, SH + 1, (8, 3)))}
def setup_inputs_zero(rng):
    d = setup_inputs(rng); s = np.zeros((8, 3), int); s[rng.integers(0, 8, 3), np.arange(3)] = SH
    d["sf"] = shifts(s); return d
def setup_inputs_most(rng):
    d = setup_inputs(rng); d["sf"] = shifts(np.full((8, 3), SH)); return d
def setup_inputs_ramp(rng):
    d = setup_inputs(rng); d["sf"] = shifts(np.stack([np.arange(8) * SH // 7] * 3, axis=1)); return d
def setup_inputs_swap(rng):
    d = setup_inputs(rng); s = rng.permutation(8) % 2 * SH
    d["sf"] = shifts(np.stack([s, SH - s, s], axis=1)); return d
def setup_inputs_spread(rng):
    d = setup_inputs(rng); d["x"] = wide(rng, N, 128, 4 * T, cols=6); return d
def check_inputs(d):
    b = []
    s = d["sf"]; g = s.reshape(N, 8, 16, 3)
    if s.min() < 0 or s.max() > SH or (g != g[:, :, :1]).any() or (s != s[:1]).any(): b.append("sf")
    if (d["w"] != d["w"][:1]).any(): b.append("w")
    return b
def reference(x, w, v, sf):
    u = [x[r] for r in range(N)]; j = np.arange(T)
    for l in range(3):
        made = []
        for r in range(N):
            s = sf[r][::16, l:l + 1]
            P = gcols(u[r], np.where(j >= s, j - s, -1))
            F = gcols(u[r - 1], np.where(j < s, T + j - s, -1)) if r > 0 else np.zeros((128, 4 * T), BF)
            qp, qf = mx_ref.quantize(P), mx_ref.quantize(F)
            R = []
            for i in range(4):
                W = mx_ref.quantize(np.ascontiguousarray(w[r][:, 2048 * l + 512 * i:2048 * l + 512 * i + 512]))
                Z = np.maximum(mx_ref.matmul(W, qp), np.float32(0)) + np.maximum(mx_ref.matmul(W, qf), np.float32(0))
                R.append(Z * np.float32(0.05))
            made.append(tile(R))
        u = made
    return {"y": np.stack([mx_ref.matmul(mx_ref.quantize(v[r]), mx_ref.quantize(u[r])) for r in range(N)])}

@@ -1,0 +1,255 @@
+from concourse.mybir import dt, AluOpType, ActivationFunctionType
+
+SCRATCH = {
+    "xu": ("sbuf", [128, 1280], "bfloat16"),
+    "g0": ("sbuf", [128, 1152], "bfloat16"),
+    "q0": ("sbuf", [128, 384], "float8_e4m3fn_x4"),
+    "s0": ("sbuf", [128, 384], "uint8"),
+    "u1": ("sbuf", [128, 1408], "bfloat16"),
+    "g1": ("sbuf", [128, 1280], "bfloat16"),
+    "q1": ("sbuf", [128, 320], "float8_e4m3fn_x4"),
+    "s1": ("sbuf", [128, 320], "uint8"),
+    "u2": ("sbuf", [128, 1280], "bfloat16"),
+    "g2": ("sbuf", [128, 1152], "bfloat16"),
+    "q2": ("sbuf", [128, 288], "float8_e4m3fn_x4"),
+    "s2": ("sbuf", [128, 288], "uint8"),
+    "u3": ("sbuf", [128, 1024], "bfloat16"),
+    "q3": ("sbuf", [128, 256], "float8_e4m3fn_x4"),
+    "s3": ("sbuf", [128, 256], "uint8"),
+    "wb": ("sbuf", [128, 6144], "bfloat16"),
+    "qw": ("sbuf", [128, 1536], "float8_e4m3fn_x4"),
+    "sw": ("sbuf", [128, 1536], "uint8"),
+    "vb": ("sbuf", [128, 512], "bfloat16"),
+    "qv": ("sbuf", [128, 128], "float8_e4m3fn_x4"),
+    "sv": ("sbuf", [128, 128], "uint8"),
+    "sft": ("sbuf", [128, 3], "int32"),
+    "step": ("sbuf", [128, 64], "int32"),
+    "part": ("sbuf", [128, 1], "int32"),
+    "low": ("sbuf", [128, 1], "int32"),
+    "lowf": ("sbuf", [128, 1], "float32"),
+    "base": ("sbuf", [128, 3], "float32"),
+    "off": ("sbuf", [128, 192], "uint16"),
+    "fp": ("sbuf", [128, 768], "float32"),
+    "fs": ("sbuf", [128, 384], "float32"),
+    "yt": ("sbuf", [128, 256], "float32"),
+    "pm": ("psum", [128, 2048], "float32"),
+    "pc": ("psum", [128, 2048], "float32"),
+}
+LOADS = ["sf", "xh", "xl", "w0a", "w0b", "w1a", "w1b", "w2a", "w2b", "v"]
+SEMAPHORES = ["qv", "qs", "qt", "qg", "rcv", "snt", "yh", "yl"] + ["ld_" + n for n in LOADS]
+SH = 32
+C = 0.05
+MAIN = ["vvss", "ssvs", "ssvs"]
+PAIR = ["ssss", "svss", "sssv"]
+HALO = ["svss", "ssvs", ""]
+REST = ["", "vsss", "ssss"]
+CUT = {"send": 256, "x": 80, "m1": 240, "m2": 200, "c2": 104}
+
+
+def rank_program(g, core, T, topo):
+    rank = T.rank_of(core)
+    if rank is None:
+        return
+    first, last = rank == 0, rank == len(T.cores) - 1
+    eng = {"v": g.vector, "s": g.scalar, "t": g.tensor, "g": g, "y": g.sync}
+    done = {"v": 0, "s": 0, "t": 0, "g": 0}
+    known = {q: {} for q in eng}
+    past = {}
+
+    def cover(a, b):
+        return a != b and past.get(a, {}).get(b[0], 0) >= b[1]
+
+    def need(q, deps):
+        best = {}
+        for s, n in deps:
+            best[s] = max(n, best.get(s, 0))
+        todo = [(s, n) for s, n in best.items() if known[q].get(s, 0) < n]
+        todo = [d for d in todo if not any(cover(e, d) for e in todo)]
+        for s, n in todo:
+            eng[q].wait_ge(T.sem[s], n)
+            for a, b in list(past.get((s, n), {}).items()) + [(s, n)]:
+                known[q][a] = max(b, known[q].get(a, 0))
+
+    def do(q, deps, call):
+        need(q, deps)
+        ins = call(eng[q])
+        done[q] += 1
+        s = "q" + q
+        ins.then_inc(T.sem[s], 1)
+        past[(s, done[q])] = dict(known[q])
+        past[(s, done[q])][s] = done[q]
+        return (s, done[q])
+
+    def dma(q, sem, deps, out, in_):
+        need(q, deps)
+        eng[q].dma_start(out, in_).then_inc(T.sem[sem], 16)
+        past[(sem, 16)] = dict(known[q])
+        return (sem, 16)
+
+    ld = {}
+    ld["sf"] = dma("y", "ld_sf", [], T.sft[:], T.sf[:])
+    ld["xh"] = dma("s", "ld_xh", [], T.xu[:, 640:1152], T.x[:, 512:1024])
+    ld["xl"] = dma("y", "ld_xl", [], T.xu[:, 128:640], T.x[:, 0:512])
+    ld["w0a"] = dma("s", "ld_w0a", [], T.wb[:, 0:1024], T.w[:, 0:1024])
+    ld["w0b"] = dma("y", "ld_w0b", [], T.wb[:, 1024:2048], T.w[:, 1024:2048])
+
+    i1 = do("g", [], lambda e: e.iota(T.part[:], [[0, 1]], 0, 1))
+    i2 = do("g", [], lambda e: e.iota(T.step[:], [[16, 64]], 0, 0))
+    zr = []
+    for ap in [T.xu[:, 1152:1280], T.xu[:, 0:128], T.u1[:, 256:384], T.u2[:, 128:256]]:
+        zr.append(do("v", [], lambda e, ap=ap: e.memset(ap, 0.0)))
+    if first:
+        zr.append(do("v", [], lambda e: e.memset(T.g1[:, 0:256], 0.0)))
+        zr.append(do("v", [], lambda e: e.memset(T.g2[:, 0:128], 0.0)))
+    t = do("v", [i1], lambda e: e.tensor_scalar(T.low[:], T.part[:], 15, None, AluOpType.bitwise_and))
+    t = do("v", [t], lambda e: e.tensor_scalar(T.lowf[:], T.low[:], 128.0, None, AluOpType.add))
+    bs = do("v", [t, ld["sf"]], lambda e: e.tensor_scalar(
+        T.base[:], T.sft[:], -4.0, T.lowf[:, 0:1], AluOpType.mult, AluOpType.add))
+
+    def lists(l):
+        return do("v", [bs, i2], lambda e: e.tensor_scalar(
+            T.off[:, 64 * l:64 * l + 64], T.step[:], T.base[:, l:l + 1], None, AluOpType.add))
+    off = {0: lists(0)}
+
+    def gather(q, l, u, gt, k0, k1, g0, deps):
+        out = gt[:, 4 * (k0 - g0):4 * (k1 - g0)]
+        win = u[:, 4 * (k0 - SH):4 * k1].indirect(T.off[:, 64 * l:64 * l + (k1 - k0) // 4])
+        if q == "v":
+            return do("v", deps + [off[l]], lambda e: e.tensor_copy(out, win))
+        return do("s", deps + [off[l]], lambda e: e.activation(out, win, ActivationFunctionType.Copy))
+
+    def quant(q, s, a, b, src, s0, deps):
+        return do("v", deps, lambda e: e.quantize_mx(q[:, a:b], s[:, a:b], src[:, 4 * s0:4 * (s0 + b - a)]))
+
+    W = {}
+
+    def quant_w(l, i0, i1, name):
+        c = 512 * l
+        t = quant(T.qw, T.sw, c + 128 * i0, c + 128 * i1, T.wb, c + 128 * i0, [ld[name]])
+        for i in range(i0, i1):
+            W[l, i] = t
+
+    def mm(ps, l, i, q, s, a, n, deps):
+        c = 512 * l + 128 * i
+        return do("t", deps + [W[l, i]], lambda e: e.matmul_mx(
+            ps[:, 512 * i:512 * i + n], T.qw[:, c:c + 128], T.sw[:, c:c + 128], q[:, a:a + n], s[:, a:a + n], True, True))
+
+    def empty(q, ps, i, a, n, u, c, deps, scale=True):
+        src = ps[:, 512 * i + a:512 * i + a + n]
+        out = u[:, 4 * c + i:4 * (c + n):4]
+        if q == "v":
+            if scale:
+                return do("v", deps, lambda e: e.tensor_scalar(out, src, 0.0, C, AluOpType.max, AluOpType.mult))
+            return do("v", deps, lambda e: e.tensor_scalar(out, src, 0.0, None, AluOpType.max))
+        f = ActivationFunctionType.Relu
+        if scale:
+            return do("s", deps, lambda e: e.activation(out, src, f, scale=C))
+        return do("s", deps, lambda e: e.activation(out, src, f))
+
+    a1 = gather("v", 0, T.xu, T.g0, 192, CUT["send"], SH, [zr[0], ld["xh"]])
+    a2 = gather("s", 0, T.xu, T.g0, CUT["send"], 320, SH, [zr[0], ld["xh"]])
+    qa = quant(T.q0, T.s0, 256, 384, T.g0, 160, [a1, a2])
+    sent = came = 0
+    if not last:
+        dst = T.cores[rank + 1]
+        rid, pid = topo.addr(dst)[0], topo.addr(dst)[1]
+        use = topo.engines(core, dst)
+        half = len(use) // 2
+        need("g", [qa])
+        g.remote_dma(T.q0[:, 0:96].bitcast(dt.uint8), T.q0[:, 288:384].bitcast(dt.uint8), T.sem.rcv, T.sem.snt, pid, rid,
+                     sum(1 << e for e in use[:half]))
+        g.remote_dma(T.s0[:, 0:96], T.s0[:, 288:384], T.sem.rcv, T.sem.snt, pid, rid, sum(1 << e for e in use[half:]))
+        sent = len(use)
+    if not first:
+        came = len(topo.engines(T.cores[rank - 1], core))
+    b1 = gather("v", 0, T.xu, T.g0, 32, CUT["x"], SH, [zr[1], ld["xl"]])
+    b2 = gather("s", 0, T.xu, T.g0, CUT["x"], 192, SH, [zr[1], ld["xl"], ld["xh"]])
+    for n, lo in [("w1a", 2048), ("w1b", 3072), ("w2a", 4096), ("w2b", 5120)]:
+        ld[n] = dma("y", "ld_" + n, [b1], T.wb[:, lo:lo + 1024], T.w[:, lo:lo + 1024])
+    ld["v"] = dma("y", "ld_v", [], T.vb[:], T.v[:])
+    quant_w(0, 0, 2, "w0a")
+    qb = quant(T.q0, T.s0, 96, 256, T.g0, 0, [b1, b2])
+    quant_w(0, 2, 4, "w0b")
+    off[1] = lists(1)
+    off[2] = lists(2)
+
+    Q = [T.q0, T.q1, T.q2]
+    S = [T.s0, T.s1, T.s2]
+    U = [None, T.u1, T.u2, T.u3]
+    own = [None, 96, 64, 0]
+    halo = [64, 32, 0]
+
+    def main_mm(l, deps):
+        return [mm(T.pm, l, i, Q[l], S[l], 128, 224 - 32 * l, deps) for i in range(4)]
+
+    def main_empty(l, tok):
+        return [empty(MAIN[l][i], T.pm, i, 0, 224 - 32 * l, U[l + 1], own[l + 1] + 32 * (l + 1), [tok[i]]) for i in range(4)]
+
+    def corner_mm(l, deps):
+        a = 96 if first and l == 0 else 0
+        return [mm(T.pc, l, i, Q[l], S[l], a, 128, deps) for i in range(4)]
+
+    def corner_empty(l, tok):
+        u, o = U[l + 1], own[l + 1]
+        p = 0 if first and l == 0 else halo[l] + 32
+        if first:
+            return [], [empty(PAIR[l][i], T.pc, i, p, 32 * (l + 1), u, o, [tok[i]]) for i in range(4)]
+        a, b = 256 * l, 128 * l
+        r = [empty(PAIR[l][i], T.pc, i, p - 32, 64, T.fp, 64 * l, [tok[i]], scale=False) for i in range(4)]
+        h, m = [], []
+        if halo[l]:
+            h = [empty(HALO[l][i], T.pc, i, 0, halo[l], u, 0, [tok[i], r[i]]) for i in range(4)]
+        if l:
+            m = [empty(REST[l][i], T.pc, i, p + 32, 32 * l, u, o + 32, [tok[i], r[i]] + h[i:i + 1]) for i in range(4)]
+        add = do("v", r, lambda e: e.tensor_tensor(
+            T.fs[:, b:b + 128], T.fp[:, a:a + 128], T.fp[:, a + 128:a + 256], AluOpType.add))
+        m.append(do("v", [add], lambda e: e.tensor_scalar(
+            u[:, 4 * o:4 * (o + 32)], T.fs[:, b:b + 128], C, None, AluOpType.mult)))
+        return h, m
+
+    tm = main_mm(0, [qa, qb])
+    tc = corner_mm(0, [qb] if first else [qb, ("rcv", came)])
+    em = main_empty(0, tm)
+    m1 = gather("v", 1, T.u1, T.g1, 160, CUT["m1"], SH, em)
+    m2 = gather("s", 1, T.u1, T.g1, CUT["m1"], 352, SH, em)
+    quant_w(1, 0, 2, "w1a")
+    qm = quant(T.q1, T.s1, 128, 320, T.g1, 128, [m1, m2])
+    quant_w(1, 2, 4, "w1b")
+    tm = main_mm(1, [qm])
+    h, m = corner_empty(0, tc)
+    c1 = [] if first else [gather("s", 1, T.u1, T.g1, 32, 96, SH, h + [zr[2]])]
+    c1.append(gather("v", 1, T.u1, T.g1, 96, 160, SH, m + em + [zr[2]]))
+    qc = quant(T.q1, T.s1, 0, 128, T.g1, 0, c1 + zr)
+    tc = corner_mm(1, [qc])
+    em = main_empty(1, tm)
+    m1 = gather("v", 2, T.u2, T.g2, 160, CUT["m2"], SH, em)
+    m2 = gather("s", 2, T.u2, T.g2, CUT["m2"], 320, SH, em)
+    quant_w(2, 0, 2, "w2a")
+    quant_w(2, 2, 4, "w2b")
+    qm = quant(T.q2, T.s2, 128, 288, T.g2, 128, [m1, m2])
+    tm = main_mm(2, [qm])
+    h, m = corner_empty(1, tc)
+    c1 = [] if first else [gather("s", 2, T.u2, T.g2, 32, 64, SH, h + [zr[3]])]
+    c1.append(gather("s", 2, T.u2, T.g2, 64, CUT["c2"], SH, m + [zr[3]]))
+    c1.append(gather("v", 2, T.u2, T.g2, CUT["c2"], 160, SH, m + em))
+    qc = quant(T.q2, T.s2, 0, 128, T.g2, 0, c1 + zr)
+    tc = corner_mm(2, [qc])
+    em = main_empty(2, tm)
+    qv = quant(T.qv, T.sv, 0, 128, T.vb, 0, [ld["v"]])
+    qh = quant(T.q3, T.s3, 128, 256, T.u3, 128, em)
+
+    def last_mm(ps, a, deps):
+        return do("t", deps, lambda e: e.matmul_mx(
+            ps[:, 0:128], T.qv[:], T.sv[:], T.q3[:, a:a + 128], T.s3[:, a:a + 128], True, True))
+    th = last_mm(T.pm, 128, [qh, qv])
+    h, m = corner_empty(2, tc)
+    ql = quant(T.q3, T.s3, 0, 128, T.u3, 0, em + m)
+    tl = last_mm(T.pc, 0, [ql])
+    yh = do("s", [th], lambda e: e.activation(T.yt[:, 128:256], T.pm[:, 0:128], ActivationFunctionType.Copy))
+    sh = dma("y", "yh", [yh], T.y[:, 128:256], T.yt[:, 128:256])
+    yl = do("v", [tl], lambda e: e.tensor_copy(T.yt[:, 0:128], T.pc[:, 0:128]))
+    sl = dma("y", "yl", [yl], T.y[:, 0:128], T.yt[:, 0:128])
+    tail = [sh, sl] + [("q" + q, n) for q, n in done.items()]
+    if not last:
+        tail.append(("snt", sent))
+    need("g", tail)

@@ -1,18 +1,19 @@
 from concourse.mybir import dt, AluOpType, ActivationFunctionType
 
 SCRATCH = {
-    "xu": ("sbuf", [128, 1280], "bfloat16"),
-    "g0": ("sbuf", [128, 1152], "bfloat16"),
-    "q0": ("sbuf", [128, 384], "float8_e4m3fn_x4"),
-    "s0": ("sbuf", [128, 384], "uint8"),
-    "u1": ("sbuf", [128, 1408], "bfloat16"),
-    "g1": ("sbuf", [128, 1280], "bfloat16"),
-    "q1": ("sbuf", [128, 320], "float8_e4m3fn_x4"),
-    "s1": ("sbuf", [128, 320], "uint8"),
-    "u2": ("sbuf", [128, 1280], "bfloat16"),
+    "xu": ("sbuf", [128, 1312], "bfloat16"),
+    "g0": ("sbuf", [128, 1696], "bfloat16"),
+    "q0": ("sbuf", [128, 424], "float8_e4m3fn_x4"),
+    "s0": ("sbuf", [128, 432], "uint8"),
+    "z1": ("sbuf", [128, 1440], "float32"),
+    "g1": ("sbuf", [128, 1312], "bfloat16"),
+    "q1": ("sbuf", [128, 328], "float8_e4m3fn_x4"),
+    "s1": ("sbuf", [128, 328], "uint8"),
+    "z2": ("sbuf", [128, 1312], "float32"),
     "g2": ("sbuf", [128, 1152], "bfloat16"),
     "q2": ("sbuf", [128, 288], "float8_e4m3fn_x4"),
     "s2": ("sbuf", [128, 288], "uint8"),
+    "z3": ("sbuf", [128, 512], "float32"),
     "u3": ("sbuf", [128, 1024], "bfloat16"),
     "q3": ("sbuf", [128, 256], "float8_e4m3fn_x4"),
     "s3": ("sbuf", [128, 256], "uint8"),
@@ -23,27 +24,28 @@ SCRATCH = {
     "qv": ("sbuf", [128, 128], "float8_e4m3fn_x4"),
     "sv": ("sbuf", [128, 128], "uint8"),
     "sft": ("sbuf", [128, 3], "int32"),
-    "step": ("sbuf", [128, 64], "int32"),
-    "part": ("sbuf", [128, 1], "int32"),
-    "low": ("sbuf", [128, 1], "int32"),
-    "lowf": ("sbuf", [128, 1], "float32"),
+    "tab": ("sbuf", [128, 128], "int32"),
+    "part": ("sbuf", [128, 2], "int32"),
+    "low": ("sbuf", [128, 1], "float32"),
     "base": ("sbuf", [128, 3], "float32"),
-    "off": ("sbuf", [128, 192], "uint16"),
-    "fp": ("sbuf", [128, 768], "float32"),
-    "fs": ("sbuf", [128, 384], "float32"),
+    "off": ("sbuf", [128, 384], "uint16"),
     "yt": ("sbuf", [128, 256], "float32"),
     "pm": ("psum", [128, 2048], "float32"),
     "pc": ("psum", [128, 2048], "float32"),
 }
-LOADS = ["sf", "xh", "xl", "w0a", "w0b", "w1a", "w1b", "w2a", "w2b", "v"]
-SEMAPHORES = ["qv", "qs", "qt", "qg", "rcv", "snt", "yh", "yl"] + ["ld_" + n for n in LOADS]
+SEMAPHORES = ["qv", "qs", "qt", "qg", "rcv", "snt", "off", "yh", "yl", "sf", "xh", "xl", "v"] + ["w%d" % i for i in range(12)]
 SH = 32
 C = 0.05
-MAIN = ["vvss", "ssvs", "ssvs"]
-PAIR = ["ssss", "svss", "sssv"]
-HALO = ["svss", "ssvs", ""]
-REST = ["", "vsss", "ssss"]
-CUT = {"send": 256, "x": 80, "m1": 240, "m2": 200, "c2": 104}
+LATE = 8
+SEND, PLAIN, FIRST, HALO, END = 0, 26, 74, 98, 116
+CFG = dict(
+    cut=dict(a=248, b=56, m1=160, m2=152, c1=64, c2=48),
+    wl=[0, 2, 4, 6, 8, 10, 12], wq=[0, 2, 4, 6, 8, 10, 12], early=4, msg="88", gates=["off"], bank="2",
+    v=("l0 l2 ga f2 qa gb w0 qb w2 w4 l1 w6 m02 f1 gm1 c01 qm1 w8 add0 m10 gc1 qc1 w10 gm2 c10 c12 qm2 add1 gc2 qc2 m22 qv qh "
+       "c21 a20 a21 a22 a23 sc ql yl").split(),
+    s="Ga Gb m00 m01 m03 Gm1 c00 c02 c03 Gh1 m11 m12 m13 Gc1 Gm2 c11 c13 Gh2 Gc2 m21 m20 m23 c20 c22 c23 rest yh".split(),
+    t="M00 M01 M02 M03 C00 C01 C02 C03 M10 M11 M12 M13 C10 C11 C12 C13 M20 M21 M22 M23 C20 C21 C22 C23 H L".split(),
+)
 
 
 def rank_program(g, core, T, topo):
@@ -55,6 +57,7 @@ def rank_program(g, core, T, topo):
     done = {"v": 0, "s": 0, "t": 0, "g": 0}
     known = {q: {} for q in eng}
     past = {}
+    cut = CFG["cut"]
 
     def cover(a, b):
         return a != b and past.get(a, {}).get(b[0], 0) >= b[1]
@@ -86,170 +89,177 @@ def rank_program(g, core, T, topo):
         past[(sem, 16)] = dict(known[q])
         return (sem, 16)
 
-    ld = {}
-    ld["sf"] = dma("y", "ld_sf", [], T.sft[:], T.sf[:])
-    ld["xh"] = dma("s", "ld_xh", [], T.xu[:, 640:1152], T.x[:, 512:1024])
-    ld["xl"] = dma("y", "ld_xl", [], T.xu[:, 128:640], T.x[:, 0:512])
-    ld["w0a"] = dma("s", "ld_w0a", [], T.wb[:, 0:1024], T.w[:, 0:1024])
-    ld["w0b"] = dma("y", "ld_w0b", [], T.wb[:, 1024:2048], T.w[:, 1024:2048])
+    k = {}
+    runs = lambda ends: list(zip(ends[:-1], ends[1:]))
 
-    i1 = do("g", [], lambda e: e.iota(T.part[:], [[0, 1]], 0, 1))
-    i2 = do("g", [], lambda e: e.iota(T.step[:], [[16, 64]], 0, 0))
-    zr = []
-    for ap in [T.xu[:, 1152:1280], T.xu[:, 0:128], T.u1[:, 256:384], T.u2[:, 128:256]]:
-        zr.append(do("v", [], lambda e, ap=ap: e.memset(ap, 0.0)))
-    if first:
-        zr.append(do("v", [], lambda e: e.memset(T.g1[:, 0:256], 0.0)))
-        zr.append(do("v", [], lambda e: e.memset(T.g2[:, 0:128], 0.0)))
-    t = do("v", [i1], lambda e: e.tensor_scalar(T.low[:], T.part[:], 15, None, AluOpType.bitwise_and))
-    t = do("v", [t], lambda e: e.tensor_scalar(T.lowf[:], T.low[:], 128.0, None, AluOpType.add))
-    bs = do("v", [t, ld["sf"]], lambda e: e.tensor_scalar(
-        T.base[:], T.sft[:], -4.0, T.lowf[:, 0:1], AluOpType.mult, AluOpType.add))
+    def load_w(a, b, deps):
+        t = dma("y", "w%d" % a, deps, T.wb[:, 512 * a:512 * b], T.w[:, 512 * a:512 * b])
+        for i in range(a, b):
+            k["ld%d" % i] = [t]
 
-    def lists(l):
-        return do("v", [bs, i2], lambda e: e.tensor_scalar(
-            T.off[:, 64 * l:64 * l + 64], T.step[:], T.base[:, l:l + 1], None, AluOpType.add))
-    off = {0: lists(0)}
+    k["sf"] = [dma("y", "sf", [], T.sft[:], T.sf[:])]
+    k["xh"] = [dma("s", "xh", [], T.xu[:, 768:1152], T.x[:, 640:1024])]
+    k["xl"] = [dma("y", "xl", [], T.xu[:, 128:768], T.x[:, 0:640])]
+    for a, b in runs(CFG["wl"])[:CFG["early"]]:
+        load_w(a, b, [])
 
-    def gather(q, l, u, gt, k0, k1, g0, deps):
-        out = gt[:, 4 * (k0 - g0):4 * (k1 - g0)]
-        win = u[:, 4 * (k0 - SH):4 * k1].indirect(T.off[:, 64 * l:64 * l + (k1 - k0) // 4])
-        if q == "v":
-            return do("v", deps + [off[l]], lambda e: e.tensor_copy(out, win))
-        return do("s", deps + [off[l]], lambda e: e.activation(out, win, ActivationFunctionType.Copy))
+    table = [(SEND, 16, 128, 16), (SEND + 17, 9, 384, 16), (PLAIN, 48, 128, 16),
+             (FIRST, 24, 16, 16), (HALO, 8, 128, 16), (HALO + 8, 1, 512, 0), (HALO + 9, 9, 256, 16)]
+    i1 = do("g", [], lambda e: e.iota(T.part[:, 0:1], [[0, 1]], 0, 1))
+    tab = [do("g", [], lambda e: e.iota(T.tab[:, a:a + n], [[s, n]], b, 0)) for a, n, b, s in table]
+    do("v", [], lambda e: e.memset(T.tab[:, SEND + 16:SEND + 17], 512))
+    do("v", [], lambda e: e.memset(T.xu[:, 1152:1312], 0.0))
+    t = do("v", [i1], lambda e: e.tensor_scalar(T.part[:, 1:2], T.part[:, 0:1], 15, None, AluOpType.bitwise_and))
+    fills = [T.xu[:, 0:128], T.g0[:, 1584:1696], T.g1[:, 272:288]] + ([T.g0[:, 0:416]] if first else [])
+    for ap in fills:
+        do("v", [], lambda e: e.memset(ap, 0.0))
+    k["zeros"] = [do("v", [t], lambda e: e.tensor_copy(T.low[:], T.part[:, 1:2]))]
+    k["base"] = [do("v", k["zeros"] + k["sf"], lambda e: e.tensor_scalar(
+        T.base[:], T.sft[:], -4.0, T.low[:, 0:1], AluOpType.mult, AluOpType.add))]
+    k["tab0"], k["tab1"], k["tab2"], k["tab"] = tab[2:3], tab[3:4], tab[4:5], tab[-1:]
 
-    def quant(q, s, a, b, src, s0, deps):
-        return do("v", deps, lambda e: e.quantize_mx(q[:, a:b], s[:, a:b], src[:, 4 * s0:4 * (s0 + b - a)]))
+    Q, S, G = [T.q0, T.q1, T.q2], [T.s0, T.s1, T.s2], [T.g0, T.g1, T.g2]
+    U = [T.xu, T.z1, T.z2, T.z3]
+    own = [32, 104, 72, 32]
+    at = [104, 72, 32]
+    Copy, Relu = ActivationFunctionType.Copy, ActivationFunctionType.Relu
 
-    W = {}
+    def lists(q, d, l, a, b, frm, bound, op):
+        return [do(q, d, lambda e: e.tensor_scalar(
+            T.off[:, 128 * l + a:128 * l + b], T.tab[:, frm:frm + b - a], T.base[:, l:l + 1], bound, AluOpType.add, op))]
 
-    def quant_w(l, i0, i1, name):
-        c = 512 * l
-        t = quant(T.qw, T.sw, c + 128 * i0, c + 128 * i1, T.wb, c + 128 * i0, [ld[name]])
-        for i in range(i0, i1):
-            W[l, i] = t
+    def pick(q, d, l, a, n, w0, w1, lst):
+        if n == 0:
+            return []
+        out = G[l][:, 4 * a:4 * (a + n)]
+        win = U[l][:, 4 * w0:4 * w1].indirect(T.off[:, 128 * l + lst:128 * l + lst + n // 4])
+        if q == "s":
+            return [do(q, d, lambda e: e.activation(out, win, Copy, scale=C if l else 1.0))]
+        if l == 0:
+            return [do(q, d, lambda e: e.tensor_copy(out, win))]
+        return [do(q, d, lambda e: e.tensor_scalar(out, win, C, None, AluOpType.mult))]
 
-    def mm(ps, l, i, q, s, a, n, deps):
-        c = 512 * l + 128 * i
-        return do("t", deps + [W[l, i]], lambda e: e.matmul_mx(
-            ps[:, 512 * i:512 * i + n], T.qw[:, c:c + 128], T.sw[:, c:c + 128], q[:, a:a + n], s[:, a:a + n], True, True))
+    def gather(q, d, l, j0, j1):
+        if l and j0 == 0:
+            return pick(q, d, l, at[l], j1, own[l] - 4, own[l] + j1, FIRST)
+        return pick(q, d, l, at[l] + j0, j1 - j0, own[l] + j0 - SH, own[l] + j1, PLAIN)
 
-    def empty(q, ps, i, a, n, u, c, deps, scale=True):
-        src = ps[:, 512 * i + a:512 * i + a + n]
-        out = u[:, 4 * c + i:4 * (c + n):4]
-        if q == "v":
-            if scale:
-                return do("v", deps, lambda e: e.tensor_scalar(out, src, 0.0, C, AluOpType.max, AluOpType.mult))
-            return do("v", deps, lambda e: e.tensor_scalar(out, src, 0.0, None, AluOpType.max))
-        f = ActivationFunctionType.Relu
+    def quant(q, d, codes, plane, tile, a, b):
+        o = LATE if plane is T.s0 else 0
+        return [do(q, d, lambda e: e.quantize_mx(codes[:, a:b], plane[:, o + a:o + b], tile[:, 4 * a:4 * b]))]
+
+    def product(q, d, ps, l, i, a, n):
+        c, o = 512 * l + 128 * i, a + (LATE if l == 0 else 0)
+        return [do(q, d, lambda e: e.matmul_mx(
+            ps[:, 512 * i:512 * i + n], T.qw[:, c:c + 128], T.sw[:, c:c + 128], Q[l][:, a:a + n], S[l][:, o:o + n], True, True))]
+
+    def empty(q, d, src, out, scale):
+        if q == "s":
+            return [do(q, d, lambda e: e.activation(out, src, Relu, scale=C if scale else 1.0))]
         if scale:
-            return do("s", deps, lambda e: e.activation(out, src, f, scale=C))
-        return do("s", deps, lambda e: e.activation(out, src, f))
+            return [do(q, d, lambda e: e.tensor_scalar(out, src, 0.0, C, AluOpType.max, AluOpType.mult))]
+        return [do(q, d, lambda e: e.tensor_scalar(out, src, 0.0, None, AluOpType.max))]
 
-    a1 = gather("v", 0, T.xu, T.g0, 192, CUT["send"], SH, [zr[0], ld["xh"]])
-    a2 = gather("s", 0, T.xu, T.g0, CUT["send"], 320, SH, [zr[0], ld["xh"]])
-    qa = quant(T.q0, T.s0, 256, 384, T.g0, 160, [a1, a2])
-    sent = came = 0
-    if not last:
-        dst = T.cores[rank + 1]
-        rid, pid = topo.addr(dst)[0], topo.addr(dst)[1]
-        use = topo.engines(core, dst)
-        half = len(use) // 2
-        need("g", [qa])
-        g.remote_dma(T.q0[:, 0:96].bitcast(dt.uint8), T.q0[:, 288:384].bitcast(dt.uint8), T.sem.rcv, T.sem.snt, pid, rid,
-                     sum(1 << e for e in use[:half]))
-        g.remote_dma(T.s0[:, 0:96], T.s0[:, 288:384], T.sem.rcv, T.sem.snt, pid, rid, sum(1 << e for e in use[half:]))
-        sent = len(use)
-    if not first:
-        came = len(topo.engines(T.cores[rank - 1], core))
-    b1 = gather("v", 0, T.xu, T.g0, 32, CUT["x"], SH, [zr[1], ld["xl"]])
-    b2 = gather("s", 0, T.xu, T.g0, CUT["x"], 192, SH, [zr[1], ld["xl"], ld["xh"]])
-    for n, lo in [("w1a", 2048), ("w1b", 3072), ("w2a", 4096), ("w2b", 5120)]:
-        ld[n] = dma("y", "ld_" + n, [b1], T.wb[:, lo:lo + 1024], T.w[:, lo:lo + 1024])
-    ld["v"] = dma("y", "ld_v", [], T.vb[:], T.v[:])
-    quant_w(0, 0, 2, "w0a")
-    qb = quant(T.q0, T.s0, 96, 256, T.g0, 0, [b1, b2])
-    quant_w(0, 2, 4, "w0b")
-    off[1] = lists(1)
-    off[2] = lists(2)
+    def add(q, d, p, f):
+        return [do(q, d, lambda e: e.tensor_tensor(p, p, f, AluOpType.add))]
 
-    Q = [T.q0, T.q1, T.q2]
-    S = [T.s0, T.s1, T.s2]
-    U = [None, T.u1, T.u2, T.u3]
-    own = [None, 96, 64, 0]
-    halo = [64, 32, 0]
+    def scale(q, d, out, src):
+        if q == "s":
+            return [do(q, d, lambda e: e.activation(out, src, Copy, scale=C))]
+        return [do(q, d, lambda e: e.tensor_scalar(out, src, C, None, AluOpType.mult))]
 
-    def main_mm(l, deps):
-        return [mm(T.pm, l, i, Q[l], S[l], 128, 224 - 32 * l, deps) for i in range(4)]
+    def last_mm(q, d, ps, a):
+        return [do(q, d, lambda e: e.matmul_mx(
+            ps[:, 0:128], T.qv[:], T.sv[:], T.q3[:, a:a + 128], T.s3[:, a:a + 128], True, True))]
 
-    def main_empty(l, tok):
-        return [empty(MAIN[l][i], T.pm, i, 0, 224 - 32 * l, U[l + 1], own[l + 1] + 32 * (l + 1), [tok[i]]) for i in range(4)]
+    def store(q, d, ps, a, sem):
+        if q == "s":
+            t = do(q, d, lambda e: e.activation(T.yt[:, a:a + 128], ps[:, 0:128], Copy))
+        else:
+            t = do(q, d, lambda e: e.tensor_copy(T.yt[:, a:a + 128], ps[:, 0:128]))
+        return [dma("y", sem, [t], T.y[:, a:a + 128], T.yt[:, a:a + 128])]
 
-    def corner_mm(l, deps):
-        a = 96 if first and l == 0 else 0
-        return [mm(T.pc, l, i, Q[l], S[l], a, 128, deps) for i in range(4)]
+    nc, ns = int(CFG["msg"][0], 17), int(CFG["msg"][1], 17)
 
-    def corner_empty(l, tok):
-        u, o = U[l + 1], own[l + 1]
-        p = 0 if first and l == 0 else halo[l] + 32
-        if first:
-            return [], [empty(PAIR[l][i], T.pc, i, p, 32 * (l + 1), u, o, [tok[i]]) for i in range(4)]
-        a, b = 256 * l, 128 * l
-        r = [empty(PAIR[l][i], T.pc, i, p - 32, 64, T.fp, 64 * l, [tok[i]], scale=False) for i in range(4)]
-        h, m = [], []
-        if halo[l]:
-            h = [empty(HALO[l][i], T.pc, i, 0, halo[l], u, 0, [tok[i], r[i]]) for i in range(4)]
+    def send(q, d):
+        qa = quant(q, d, T.q0, T.s0, T.g0, 296, 424)
+        if not last:
+            dst = T.cores[rank + 1]
+            rid, pid = topo.addr(dst)[0], topo.addr(dst)[1]
+            use = topo.engines(core, dst)
+            need("g", qa)
+            g.remote_dma(T.q0[:, 0:104].bitcast(dt.uint8), T.q0[:, 296:400].bitcast(dt.uint8), T.sem.rcv, T.sem.snt, pid, rid,
+                         sum(1 << e for e in use[:nc]))
+            g.remote_dma(T.s0[:, LATE:LATE + 104], T.s0[:, LATE + 296:LATE + 400], T.sem.rcv, T.sem.snt, pid, rid,
+                         sum(1 << e for e in use[-ns:]))
+            if "off" in " ".join(CFG["gates"]):
+                g.sem_inc(T.sem.off, 1)
+        k.update(qa=qa, none=[], off=qa if last else [("off", 1)], snt=qa if last else [("snt", nc + ns)])
+        late = runs(CFG["wl"])[CFG["early"]:] + [None]
+        for j, r in enumerate(late):
+            gate = [t for n in CFG["gates"][min(j, len(CFG["gates"]) - 1)].split("+") for t in k[n]]
+            if r:
+                load_w(r[0], r[1], gate)
+            else:
+                k["v"] = [dma("y", "v", gate, T.vb[:], T.v[:])]
+        return qa
+
+    k["rcv"] = [] if first else [("rcv", nc + ns)]
+    M = [["m%d%d" % (l, i) for i in range(4)] for l in range(3)]
+    K = [["c%d%d" % (l, i) for i in range(4)] for l in range(3)]
+    A = [["a%d%d" % (l, i) for i in range(4)] if str(l) in CFG["bank"] else ["add%d" % l] for l in range(3)]
+    a = cut["a"]
+    steps = {
+        "l0": (["base", "tab0"], lists, 0, SEND, FIRST, SEND, 0.0, AluOpType.max),
+        "ga": (["l0", "zeros", "xh"], pick, 0, at[0] + 192, a - 192, 192, 328, SEND),
+        "Ga": (["l0", "zeros", "xh"], pick, 0, at[0] + a, 292 - a, 192, 328, SEND + (a - 192) // 4),
+        "gb": (["l0", "zeros", "xl"], gather, 0, 0, cut["b"]), "Gb": (["l0", "zeros", "xl", "xh"], gather, 0, cut["b"], 192),
+        "qa": (["ga", "Ga"], send), "qb": (["gb", "Gb"], quant, T.q0, T.s0, T.g0, 0 if first else 104, 296),
+        "f1": (["base", "tab"], lists, 1, HALO, END, HALO, 256.0, AluOpType.min),
+        "f2": (["base", "tab2"], lists, 2, HALO, HALO + 8, HALO, 128.0, AluOpType.min),
+        "Gh1": (K[0] + ["f1"], pick, 1, 0, 68, 0, 68, HALO), "Gh2": (K[1] + ["f2"], pick, 2, 0, 32, 0, 36, HALO),
+        "qv": (["v"], quant, T.qv, T.sv, T.vb, 0, 128),
+        "sc": (A[2], scale, T.u3[:, 0:128], T.z3[:, 128:256]), "rest": (K[2], scale, T.u3[:, 128:384], T.z3[:, 256:512]),
+        "all": (A[2], scale, T.u3[:, 0:384], T.z3[:, 128:512]),
+        "qh": (M[2], quant, T.q3, T.s3, T.u3, 128, 256),
+        "ql": (M[2] + (["all"] if "all" in CFG["v"] + CFG["s"] else ["sc", "rest"]), quant, T.q3, T.s3, T.u3, 0, 128),
+        "H": (["qh", "qv"], last_mm, T.pm, 128), "L": (["ql", "qv"], last_mm, T.pc, 0),
+        "yh": (["H"], store, T.pm, 128, "yh"), "yl": (["L"], store, T.pc, 0, "yl"),
+    }
+    W = {}
+    for a, b in runs(CFG["wq"]):
+        steps["w%d" % a] = (["ld%d" % i for i in range(a, b)], quant, T.qw, T.sw, T.wb, 128 * a, 128 * b)
+        W.update({i: "w%d" % a for i in range(a, b)})
+    for l in range(3):
+        z, o, p = U[l + 1], 4 * own[l + 1], 32 * (l + 1)
+        f, n = o - (128 if l == 2 else 144), at[l] + p
+        steps["add%d" % l] = (K[l], add, z[:, o:o + 128], z[:, f:f + 128])
+        for i in range(4):
+            u, c = (T.u3, 4 * p) if l == 2 else (z, o + 4 * p)
+            steps["a%d%d" % (l, i)] = ([K[l][i]], add, z[:, o + i:o + 128:4], z[:, f + i:f + 128:4])
+            steps["M%d%d" % (l, i)] = ((["qm%d" % l] if l else ["qa", "qb"]) + [W[4 * l + i]], product, T.pm, l, i, n, 256 - p)
+            steps["C%d%d" % (l, i)] = ((["qc%d" % l] if l else ["qb", "rcv"]) + [W[4 * l + i]], product, T.pc, l, i, 0, n)
+            steps[M[l][i]] = (["M%d%d" % (l, i)], empty, T.pm[:, 512 * i:512 * i + 256 - p], u[:, c + i:c + 4 * (256 - p):4], l == 2)
+            steps[K[l][i]] = (["C%d%d" % (l, i)], empty, T.pc[:, 512 * i:512 * i + n], z[:, i:4 * n:4], False)
         if l:
-            m = [empty(REST[l][i], T.pc, i, p + 32, 32 * l, u, o + 32, [tok[i], r[i]] + h[i:i + 1]) for i in range(4)]
-        add = do("v", r, lambda e: e.tensor_tensor(
-            T.fs[:, b:b + 128], T.fp[:, a:a + 128], T.fp[:, a + 128:a + 256], AluOpType.add))
-        m.append(do("v", [add], lambda e: e.tensor_scalar(
-            u[:, 4 * o:4 * (o + 32)], T.fs[:, b:b + 128], C, None, AluOpType.mult)))
-        return h, m
-
-    tm = main_mm(0, [qa, qb])
-    tc = corner_mm(0, [qb] if first else [qb, ("rcv", came)])
-    em = main_empty(0, tm)
-    m1 = gather("v", 1, T.u1, T.g1, 160, CUT["m1"], SH, em)
-    m2 = gather("s", 1, T.u1, T.g1, CUT["m1"], 352, SH, em)
-    quant_w(1, 0, 2, "w1a")
-    qm = quant(T.q1, T.s1, 128, 320, T.g1, 128, [m1, m2])
-    quant_w(1, 2, 4, "w1b")
-    tm = main_mm(1, [qm])
-    h, m = corner_empty(0, tc)
-    c1 = [] if first else [gather("s", 1, T.u1, T.g1, 32, 96, SH, h + [zr[2]])]
-    c1.append(gather("v", 1, T.u1, T.g1, 96, 160, SH, m + em + [zr[2]]))
-    qc = quant(T.q1, T.s1, 0, 128, T.g1, 0, c1 + zr)
-    tc = corner_mm(1, [qc])
-    em = main_empty(1, tm)
-    m1 = gather("v", 2, T.u2, T.g2, 160, CUT["m2"], SH, em)
-    m2 = gather("s", 2, T.u2, T.g2, CUT["m2"], 320, SH, em)
-    quant_w(2, 0, 2, "w2a")
-    quant_w(2, 2, 4, "w2b")
-    qm = quant(T.q2, T.s2, 128, 288, T.g2, 128, [m1, m2])
-    tm = main_mm(2, [qm])
-    h, m = corner_empty(1, tc)
-    c1 = [] if first else [gather("s", 2, T.u2, T.g2, 32, 64, SH, h + [zr[3]])]
-    c1.append(gather("s", 2, T.u2, T.g2, 64, CUT["c2"], SH, m + [zr[3]]))
-    c1.append(gather("v", 2, T.u2, T.g2, CUT["c2"], 160, SH, m + em))
-    qc = quant(T.q2, T.s2, 0, 128, T.g2, 0, c1 + zr)
-    tc = corner_mm(2, [qc])
-    em = main_empty(2, tm)
-    qv = quant(T.qv, T.sv, 0, 128, T.vb, 0, [ld["v"]])
-    qh = quant(T.q3, T.s3, 128, 256, T.u3, 128, em)
-
-    def last_mm(ps, a, deps):
-        return do("t", deps, lambda e: e.matmul_mx(
-            ps[:, 0:128], T.qv[:], T.sv[:], T.q3[:, a:a + 128], T.s3[:, a:a + 128], True, True))
-    th = last_mm(T.pm, 128, [qh, qv])
-    h, m = corner_empty(2, tc)
-    ql = quant(T.q3, T.s3, 0, 128, T.u3, 0, em + m)
-    tl = last_mm(T.pc, 0, [ql])
-    yh = do("s", [th], lambda e: e.activation(T.yt[:, 128:256], T.pm[:, 0:128], ActivationFunctionType.Copy))
-    sh = dma("y", "yh", [yh], T.y[:, 128:256], T.yt[:, 128:256])
-    yl = do("v", [tl], lambda e: e.tensor_copy(T.yt[:, 0:128], T.pc[:, 0:128]))
-    sl = dma("y", "yl", [yl], T.y[:, 0:128], T.yt[:, 0:128])
-    tail = [sh, sl] + [("q" + q, n) for q, n in done.items()]
+            a, b, d = cut["m%d" % l], cut["c%d" % l], M[l - 1] + ["l%d" % l]
+            steps["l%d" % l] = (["base", "tab1"], lists, l, PLAIN, HALO, PLAIN, 0.0, AluOpType.max)
+            steps["gm%d" % l] = (d, gather, l, p, a)
+            steps["Gm%d" % l] = (d, gather, l, a, 256)
+            steps["gc%d" % l] = (d + A[l - 1], gather, l, 0, b)
+            steps["Gc%d" % l] = (d + A[l - 1], gather, l, b, p)
+            steps["qm%d" % l] = (["gm%d" % l, "Gm%d" % l], quant, Q[l], S[l], G[l], n, at[l] + 256)
+            steps["qc%d" % l] = (["gc%d" % l, "Gc%d" % l, "Gh%d" % l, "zeros"], quant, Q[l], S[l], G[l], 0, n)
+    todo = {q: list(CFG[q]) for q in "vst"}
+    while any(todo.values()):
+        moved = False
+        for q in todo:
+            while todo[q] and all(d in k for d in steps[todo[q][0]][0]):
+                n = todo[q].pop(0)
+                k[n] = steps[n][1](q, [t for d in steps[n][0] for t in k[d]], *steps[n][2:])
+                moved = True
+        assert moved, todo
+    tail = k["yh"] + k["yl"] + [("q" + q, n) for q, n in done.items()]
     if not last:
-        tail.append(("snt", sent))
+        tail.append(("snt", nc + ns))
     need("g", tail)

@@ -14,9 +14,14 @@ SCRATCH = {
     "q2": ("sbuf", [128, 288], "float8_e4m3fn_x4"),
     "s2": ("sbuf", [128, 288], "uint8"),
     "z3": ("sbuf", [128, 512], "float32"),
-    "u3": ("sbuf", [128, 1024], "bfloat16"),
-    "q3": ("sbuf", [128, 256], "float8_e4m3fn_x4"),
-    "s3": ("sbuf", [128, 256], "uint8"),
+    "u3": ("sbuf", [128, 1152], "bfloat16"),
+    "tabq": ("sbuf", [128, 48], "float32"),
+    "q3": ("sbuf", [128, 128], "float8_e4m3fn_x4"),
+    "s3": ("sbuf", [128, 128], "uint8"),
+    "q4": ("sbuf", [128, 160], "float8_e4m3fn_x4"),
+    "s4": ("sbuf", [128, 160], "uint8"),
+    "qs": ("sbuf", [128, 128], "float8_e4m3fn_x4"),
+    "ss": ("sbuf", [128, 128], "uint8"),
     "wb": ("sbuf", [128, 6144], "bfloat16"),
     "qw": ("sbuf", [128, 1536], "float8_e4m3fn_x4"),
     "sw": ("sbuf", [128, 1536], "uint8"),
@@ -37,13 +42,14 @@ SEMAPHORES = ["qv", "qs", "qt", "qg", "rcv", "snt", "off", "yh", "yl", "sf", "xh
 SH = 32
 C = 0.05
 LATE = 8
-SEND, PLAIN, FIRST, HALO, END = 0, 26, 74, 98, 116
+PLAIN, FIRST, HALO, END = 0, 48, 72, 90
 CFG = dict(
-    cut=dict(a=248, b=56, m1=160, m2=152, c1=64, c2=48),
-    wl=[0, 2, 4, 6, 8, 10, 12], wq=[0, 2, 4, 6, 8, 10, 12], early=4, msg="88", gates=["off"], bank="2",
-    v=("l0 l2 ga f2 qa gb w0 qb w2 w4 l1 w6 m02 f1 gm1 c01 qm1 w8 add0 m10 gc1 qc1 w10 gm2 c10 c12 qm2 add1 gc2 qc2 m22 qv qh "
-       "c21 a20 a21 a22 a23 sc ql yl").split(),
-    s="Ga Gb m00 m01 m03 Gm1 c00 c02 c03 Gh1 m11 m12 m13 Gc1 Gm2 c11 c13 Gh2 Gc2 m21 m20 m23 c20 c22 c23 rest yh".split(),
+    cut=dict(a=256, b=48, m1=160, m2=200, c1=40, c2=48),
+    wl=[0, 2, 4, 6, 8, 10, 12], wq=[0, 2, 4, 6, 8, 10, 12], early=4, qx="s", msg="88", gates=["off"], bank="2", halves=False, xcut=160,
+    v=("l0 base ga qa gb w0 qb w2 l1 f1 f2 w4 l2 m02 w6 gm1 c01 qm1 w8 add0 m10 Gc1 m12 qc1 w10 gm2 c12 qm2 add1 gc2 qc2 m22 qv qh "
+       "a20 a21 a22 a23 sc ql yl").split(),
+    s=("Ga Gy Gb m00 m01 m03 Gm1 c00 c02 c03 Gh1 gc1 m11 m13 Gm2 c10 c11 c13 Gh2 Gc2 m21 m20 m23 c20 c21 c22 c23 "
+       "r20 r21 r22 r23 yh").split(),
     t="M00 M01 M02 M03 C00 C01 C02 C03 M10 M11 M12 M13 C10 C11 C12 C13 M20 M21 M22 M23 C20 C21 C22 C23 H L".split(),
 )
 
@@ -98,25 +104,34 @@ def rank_program(g, core, T, topo):
             k["ld%d" % i] = [t]
 
     k["sf"] = [dma("y", "sf", [], T.sft[:], T.sf[:])]
-    k["xh"] = [dma("s", "xh", [], T.xu[:, 768:1152], T.x[:, 640:1024])]
-    k["xl"] = [dma("y", "xl", [], T.xu[:, 128:768], T.x[:, 0:640])]
+    xc = 4 * CFG["xcut"]
+    k["xh"] = [dma(CFG["qx"], "xh", [], T.xu[:, 128 + xc:1152], T.x[:, xc:1024])]
+    k["xl"] = [dma("y", "xl", [], T.xu[:, 128:128 + xc], T.x[:, 0:xc])]
     for a, b in runs(CFG["wl"])[:CFG["early"]]:
         load_w(a, b, [])
 
-    table = [(SEND, 16, 128, 16), (SEND + 17, 9, 384, 16), (PLAIN, 48, 128, 16),
-             (FIRST, 24, 16, 16), (HALO, 8, 128, 16), (HALO + 8, 1, 512, 0), (HALO + 9, 9, 256, 16)]
+    table = [(PLAIN, 48, 128, 16), (FIRST, 24, 16, 16),
+             (HALO, 8, 128, 16), (HALO + 8, 1, 512, 0), (HALO + 9, 9, 256, 16)]
     i1 = do("g", [], lambda e: e.iota(T.part[:, 0:1], [[0, 1]], 0, 1))
     tab = [do("g", [], lambda e: e.iota(T.tab[:, a:a + n], [[s, n]], b, 0)) for a, n, b, s in table]
-    do("v", [], lambda e: e.memset(T.tab[:, SEND + 16:SEND + 17], 512))
-    do("v", [], lambda e: e.memset(T.xu[:, 1152:1312], 0.0))
-    t = do("v", [i1], lambda e: e.tensor_scalar(T.part[:, 1:2], T.part[:, 0:1], 15, None, AluOpType.bitwise_and))
-    fills = [T.xu[:, 0:128], T.g0[:, 1584:1696], T.g1[:, 272:288]] + ([T.g0[:, 0:416]] if first else [])
-    for ap in fills:
-        do("v", [], lambda e: e.memset(ap, 0.0))
-    k["zeros"] = [do("v", [t], lambda e: e.tensor_copy(T.low[:], T.part[:, 1:2]))]
-    k["base"] = [do("v", k["zeros"] + k["sf"], lambda e: e.tensor_scalar(
-        T.base[:], T.sft[:], -4.0, T.low[:, 0:1], AluOpType.mult, AluOpType.add))]
-    k["tab0"], k["tab1"], k["tab2"], k["tab"] = tab[2:3], tab[3:4], tab[4:5], tab[-1:]
+    k["tab1"], k["tab2"], k["tab"] = tab[1:2], tab[2:3], tab[-1:]
+
+    def zero(buf, a, b):
+        return do("g", [], lambda e: e.iota(buf[:, a:b], [[0, b - a]], 0, 0, allow_small_or_imprecise_dtypes=True))
+    k["pad"] = [zero(T.g1, 272, 288), zero(T.u3, 384, 512)][-1:]
+    do("v", [], lambda e: e.memset(T.xu[:, 1152:1280], 0.0))
+    do("v", [], lambda e: e.memset(T.g0[:, 1440:1696], 0.0))
+    low = do("v", [i1], lambda e: e.tensor_scalar(T.part[:, 1:2], T.part[:, 0:1], 15, None, AluOpType.bitwise_and))
+    do("v", [], lambda e: e.memset(T.xu[:, 0:128], 0.0))
+    k["zeros"] = [do("v", [low, tab[0]], lambda e: e.tensor_scalar(
+        T.tabq[:], T.tab[:, PLAIN:FIRST], T.part[:, 1:2], 0.25, AluOpType.add, AluOpType.mult))]
+
+    def list0(q, d):
+        return [do(q, d, lambda e: e.tensor_scalar(
+            T.off[:, PLAIN:FIRST], T.tabq[:], T.sft[:, 0:1], 4.0, AluOpType.subtract, AluOpType.mult))]
+
+    def base(q, d):
+        return [do(q, d, lambda e: e.tensor_scalar(T.base[:], T.sft[:], -4.0, T.part[:, 1:2], AluOpType.mult, AluOpType.add))]
 
     Q, S, G = [T.q0, T.q1, T.q2], [T.s0, T.s1, T.s2], [T.g0, T.g1, T.g2]
     U = [T.xu, T.z1, T.z2, T.z3]
@@ -168,30 +183,36 @@ def rank_program(g, core, T, topo):
             return [do(q, d, lambda e: e.activation(out, src, Copy, scale=C))]
         return [do(q, d, lambda e: e.tensor_scalar(out, src, C, None, AluOpType.mult))]
 
-    def last_mm(q, d, ps, a):
-        return [do(q, d, lambda e: e.matmul_mx(
-            ps[:, 0:128], T.qv[:], T.sv[:], T.q3[:, a:a + 128], T.s3[:, a:a + 128], True, True))]
+    def last_mm(q, d, ps, codes, plane, n):
+        return [do(q, d, lambda e: e.matmul_mx(ps[:, 0:n], T.qv[:], T.sv[:], codes[:, 0:n], plane[:, 0:n], True, True))]
 
-    def store(q, d, ps, a, sem):
+    def quant_high(q, d):
+        return [do(q, d, lambda e: e.quantize_mx(T.q4[:], T.s4[:], T.u3[:, 512:1152]))]
+
+    def store(q, d, ps, a, b, sem):
         if q == "s":
-            t = do(q, d, lambda e: e.activation(T.yt[:, a:a + 128], ps[:, 0:128], Copy))
+            t = do(q, d, lambda e: e.activation(T.yt[:, a:b], ps[:, 0:b - a], Copy))
         else:
-            t = do(q, d, lambda e: e.tensor_copy(T.yt[:, a:a + 128], ps[:, 0:128]))
-        return [dma("y", sem, [t], T.y[:, a:a + 128], T.yt[:, a:a + 128])]
+            t = do(q, d, lambda e: e.tensor_copy(T.yt[:, a:b], ps[:, 0:b - a]))
+        return [dma("y", sem, [t], T.y[:, a:b], T.yt[:, a:b])]
 
     nc, ns = int(CFG["msg"][0], 17), int(CFG["msg"][1], 17)
 
     def send(q, d):
-        qa = quant(q, d, T.q0, T.s0, T.g0, 296, 424)
+        if CFG["halves"]:
+            qa = [] if last else [do(q, d, lambda e: e.quantize_mx(T.qs[:], T.ss[:], T.g0[:, 1184:1696]))]
+            codes, plane = T.qs[:, 0:104], T.ss[:, 0:104]
+        else:
+            qa = quant(q, d, T.q0, T.s0, T.g0, 296, 424)
+            codes, plane = T.q0[:, 296:400], T.s0[:, LATE + 296:LATE + 400]
         if not last:
             dst = T.cores[rank + 1]
             rid, pid = topo.addr(dst)[0], topo.addr(dst)[1]
             use = topo.engines(core, dst)
             need("g", qa)
-            g.remote_dma(T.q0[:, 0:104].bitcast(dt.uint8), T.q0[:, 296:400].bitcast(dt.uint8), T.sem.rcv, T.sem.snt, pid, rid,
+            g.remote_dma(T.q0[:, 0:104].bitcast(dt.uint8), codes.bitcast(dt.uint8), T.sem.rcv, T.sem.snt, pid, rid,
                          sum(1 << e for e in use[:nc]))
-            g.remote_dma(T.s0[:, LATE:LATE + 104], T.s0[:, LATE + 296:LATE + 400], T.sem.rcv, T.sem.snt, pid, rid,
-                         sum(1 << e for e in use[-ns:]))
+            g.remote_dma(T.s0[:, LATE:LATE + 104], plane, T.sem.rcv, T.sem.snt, pid, rid, sum(1 << e for e in use[-ns:]))
             if "off" in " ".join(CFG["gates"]):
                 g.sem_inc(T.sem.off, 1)
         k.update(qa=qa, none=[], off=qa if last else [("off", 1)], snt=qa if last else [("snt", nc + ns)])
@@ -202,6 +223,8 @@ def rank_program(g, core, T, topo):
                 load_w(r[0], r[1], gate)
             else:
                 k["v"] = [dma("y", "v", gate, T.vb[:], T.v[:])]
+        if first:
+            k["nil"] = [zero(T.z1, 400, 416), zero(T.g1, 0, 272), zero(T.g2, 0, 128)][-1:]
         return qa
 
     k["rcv"] = [] if first else [("rcv", nc + ns)]
@@ -210,21 +233,23 @@ def rank_program(g, core, T, topo):
     A = [["a%d%d" % (l, i) for i in range(4)] if str(l) in CFG["bank"] else ["add%d" % l] for l in range(3)]
     a = cut["a"]
     steps = {
-        "l0": (["base", "tab0"], lists, 0, SEND, FIRST, SEND, 0.0, AluOpType.max),
-        "ga": (["l0", "zeros", "xh"], pick, 0, at[0] + 192, a - 192, 192, 328, SEND),
-        "Ga": (["l0", "zeros", "xh"], pick, 0, at[0] + a, 292 - a, 192, 328, SEND + (a - 192) // 4),
-        "gb": (["l0", "zeros", "xl"], gather, 0, 0, cut["b"]), "Gb": (["l0", "zeros", "xl", "xh"], gather, 0, cut["b"], 192),
-        "qa": (["ga", "Ga"], send), "qb": (["gb", "Gb"], quant, T.q0, T.s0, T.g0, 0 if first else 104, 296),
+        "l0": (["sf", "zeros"], list0),
+        "ga": (["l0", "xh"], gather, 0, 192, a), "Gy": (["l0", "xh"], gather, 0, a, 256),
+        "Ga": (["l0", "xh"], pick, 0, at[0] + 260, 32, 256, 320, PLAIN),
+        "gb": (["l0", "xl"], gather, 0, 0, cut["b"]), "Gb": (["l0", "xl", "xh"], gather, 0, cut["b"], 192),
+        "qa": (["ga", "Ga", "Gy"], send),
+        "qb": (["gb", "Gb"], quant, T.q0, T.s0, T.g0, 104, 296),
         "f1": (["base", "tab"], lists, 1, HALO, END, HALO, 256.0, AluOpType.min),
         "f2": (["base", "tab2"], lists, 2, HALO, HALO + 8, HALO, 128.0, AluOpType.min),
         "Gh1": (K[0] + ["f1"], pick, 1, 0, 68, 0, 68, HALO), "Gh2": (K[1] + ["f2"], pick, 2, 0, 32, 0, 36, HALO),
         "qv": (["v"], quant, T.qv, T.sv, T.vb, 0, 128),
         "sc": (A[2], scale, T.u3[:, 0:128], T.z3[:, 128:256]), "rest": (K[2], scale, T.u3[:, 128:384], T.z3[:, 256:512]),
         "all": (A[2], scale, T.u3[:, 0:384], T.z3[:, 128:512]),
-        "qh": (M[2], quant, T.q3, T.s3, T.u3, 128, 256),
-        "ql": (M[2] + (["all"] if "all" in CFG["v"] + CFG["s"] else ["sc", "rest"]), quant, T.q3, T.s3, T.u3, 0, 128),
-        "H": (["qh", "qv"], last_mm, T.pm, 128), "L": (["ql", "qv"], last_mm, T.pc, 0),
-        "yh": (["H"], store, T.pm, 128, "yh"), "yl": (["L"], store, T.pc, 0, "yl"),
+        "qh": (M[2], quant_high),
+        "ql": (["pad", "sc", "rest"], quant, T.q3, T.s3, T.u3, 0, 128),
+        "base": (["zeros", "sf"], base),
+        "H": (["qh", "qv"], last_mm, T.pm, T.q4, T.s4, 160), "L": (["ql", "qv"], last_mm, T.pc, T.q3, T.s3, 128),
+        "yh": (["H"], store, T.pm, 96, 256, "yh"), "yl": (["L"], store, T.pc, 0, 96, "yl"),
     }
     W = {}
     for a, b in runs(CFG["wq"]):
@@ -235,7 +260,7 @@ def rank_program(g, core, T, topo):
         f, n = o - (128 if l == 2 else 144), at[l] + p
         steps["add%d" % l] = (K[l], add, z[:, o:o + 128], z[:, f:f + 128])
         for i in range(4):
-            u, c = (T.u3, 4 * p) if l == 2 else (z, o + 4 * p)
+            u, c = (T.u3, 512) if l == 2 else (z, o + 4 * p)
             steps["a%d%d" % (l, i)] = ([K[l][i]], add, z[:, o + i:o + 128:4], z[:, f + i:f + 128:4])
             steps["M%d%d" % (l, i)] = ((["qm%d" % l] if l else ["qa", "qb"]) + [W[4 * l + i]], product, T.pm, l, i, n, 256 - p)
             steps["C%d%d" % (l, i)] = ((["qc%d" % l] if l else ["qb", "rcv"]) + [W[4 * l + i]], product, T.pc, l, i, 0, n)
@@ -249,7 +274,34 @@ def rank_program(g, core, T, topo):
             steps["gc%d" % l] = (d + A[l - 1], gather, l, 0, b)
             steps["Gc%d" % l] = (d + A[l - 1], gather, l, b, p)
             steps["qm%d" % l] = (["gm%d" % l, "Gm%d" % l], quant, Q[l], S[l], G[l], n, at[l] + 256)
-            steps["qc%d" % l] = (["gc%d" % l, "Gc%d" % l, "Gh%d" % l, "zeros"], quant, Q[l], S[l], G[l], 0, n)
+            steps["qc%d" % l] = (["gc%d" % l, "Gc%d" % l, "Gh%d" % l, "pad"], quant, Q[l], S[l], G[l], 0, n)
+    if cut["c2"] >= 64:
+        steps["Gc2"] = (M[1] + K[1] + ["l2"],) + steps["Gc2"][1:]
+    if "r20" in CFG["v"] + CFG["s"]:
+        for i in range(4):
+            steps[K[2][i]] = (["C2%d" % i], empty, T.pc[:, 512 * i:512 * i + 64], T.z3[:, i:256:4], False)
+            steps["r2%d" % i] = ([K[2][i]], empty, T.pc[:, 512 * i + 64:512 * i + 128], T.u3[:, 128 + i:384:4], True)
+        steps["ql"] = (["pad", "sc", "r20", "r21", "r22", "r23"],) + steps["ql"][1:]
+    if CFG["halves"]:
+        steps["Gx"] = (["l0", "xh"], gather, 0, 128, 192)
+        steps["qx"] = (["ga", "Gy", "Gx"], quant, T.q0, T.s0, T.g0, 232, 360)
+        steps["Gb"] = (["l0", "xl", "xh"], gather, 0, cut["b"], 128)
+        steps["qb"] = (["gb", "Gb"], quant, T.q0, T.s0, T.g0, 104, 232)
+        N = ["n0%d" % i for i in range(4)]
+        for i in range(4):
+            steps["A0%d" % i] = (["qx", W[i]], product, T.pc, 0, i, 232, 128)
+            steps[N[i]] = (["A0%d" % i], empty, T.pc[:, 512 * i:512 * i + 128], T.z1[:, 928 + i:1440:4], False)
+            steps["M0%d" % i] = (["qx", "qb", W[i]], product, T.pm, 0, i, 136, 128)
+            steps[M[0][i]] = (["M0%d" % i], empty, T.pm[:, 512 * i:512 * i + 96], T.z1[:, 544 + i:928:4], False)
+            steps["C0%d" % i] = (["qb", "rcv", N[i], W[i]],) + steps["C0%d" % i][1:]
+        steps["gm1"] = (steps["gm1"][0] + N,) + steps["gm1"][1:]
+        steps["Gm1"] = (N + ["l1"] + (M[0] if cut["m1"] < 160 else []),) + steps["Gm1"][1:]
+    if first:
+        for i in range(4):
+            steps["C0%d" % i] = (steps["C0%d" % i][0], product, T.pc, 0, i, 104, 128)
+            steps[K[0][i]] = (["C0%d" % i], empty, T.pc[:, 512 * i:512 * i + 32], T.z1[:, 416 + i:544:4], False)
+        for n in ["f1", "f2", "Gh1", "Gh2"] + A[0] + A[1]:
+            steps[n] = (steps[n][0] + ["nil"], lambda q, d: d)
     todo = {q: list(CFG[q]) for q in "vst"}
     while any(todo.values()):
         moved = False
@@ -259,7 +311,4 @@ def rank_program(g, core, T, topo):
                 k[n] = steps[n][1](q, [t for d in steps[n][0] for t in k[d]], *steps[n][2:])
                 moved = True
         assert moved, todo
-    tail = k["yh"] + k["yl"] + [("q" + q, n) for q, n in done.items()]
-    if not last:
-        tail.append(("snt", nc + ns))
-    need("g", tail)
+    need("g", ([] if last else [("snt", nc + ns)]) + [("q" + q, n) for q, n in done.items()] + k["yh"] + k["yl"])

from concourse.mybir import dt, AluOpType, ActivationFunctionType

SCRATCH = {
    "xu": ("sbuf", [128, 1312], "bfloat16"),
    "g0": ("sbuf", [128, 1696], "bfloat16"),
    "q0": ("sbuf", [128, 424], "float8_e4m3fn_x4"),
    "s0": ("sbuf", [128, 432], "uint8"),
    "z1": ("sbuf", [128, 1440], "float32"),
    "g1": ("sbuf", [128, 1312], "bfloat16"),
    "q1": ("sbuf", [128, 328], "float8_e4m3fn_x4"),
    "s1": ("sbuf", [128, 328], "uint8"),
    "z2": ("sbuf", [128, 1312], "float32"),
    "g2": ("sbuf", [128, 1152], "bfloat16"),
    "q2": ("sbuf", [128, 288], "float8_e4m3fn_x4"),
    "s2": ("sbuf", [128, 288], "uint8"),
    "z3": ("sbuf", [128, 512], "float32"),
    "u3": ("sbuf", [128, 1152], "bfloat16"),
    "tabq": ("sbuf", [128, 48], "float32"),
    "q3": ("sbuf", [128, 128], "float8_e4m3fn_x4"),
    "s3": ("sbuf", [128, 128], "uint8"),
    "q4": ("sbuf", [128, 160], "float8_e4m3fn_x4"),
    "s4": ("sbuf", [128, 160], "uint8"),
    "qs": ("sbuf", [128, 128], "float8_e4m3fn_x4"),
    "ss": ("sbuf", [128, 128], "uint8"),
    "wb": ("sbuf", [128, 6144], "bfloat16"),
    "qw": ("sbuf", [128, 1536], "float8_e4m3fn_x4"),
    "sw": ("sbuf", [128, 1536], "uint8"),
    "vb": ("sbuf", [128, 512], "bfloat16"),
    "qv": ("sbuf", [128, 128], "float8_e4m3fn_x4"),
    "sv": ("sbuf", [128, 128], "uint8"),
    "sft": ("sbuf", [128, 3], "int32"),
    "tab": ("sbuf", [128, 128], "int32"),
    "part": ("sbuf", [128, 2], "int32"),
    "low": ("sbuf", [128, 1], "float32"),
    "base": ("sbuf", [128, 3], "float32"),
    "off": ("sbuf", [128, 384], "uint16"),
    "yt": ("sbuf", [128, 256], "float32"),
    "pm": ("psum", [128, 2048], "float32"),
    "pc": ("psum", [128, 2048], "float32"),
}
SEMAPHORES = ["qv", "qs", "qt", "qg", "rcv", "snt", "off", "yh", "yl", "sf", "xh", "xl", "v"] + ["w%d" % i for i in range(12)]
SH = 32
C = 0.05
LATE = 8
PLAIN, FIRST, HALO, END = 0, 48, 72, 90
CFG = dict(
    cut=dict(a=256, b=48, m1=160, m2=200, c1=40, c2=48),
    wl=[0, 2, 4, 6, 8, 10, 12], wq=[0, 2, 4, 6, 8, 10, 12], early=4, qx="s", msg="88", gates=["off"], bank="2", halves=False, xcut=160,
    v=("l0 base ga qa gb w0 qb w2 l1 f1 f2 w4 l2 m02 w6 gm1 c01 qm1 w8 add0 m10 Gc1 m12 qc1 w10 gm2 c12 qm2 add1 gc2 qc2 m22 qv qh "
       "a20 a21 a22 a23 sc ql yl").split(),
    s=("Ga Gy Gb m00 m01 m03 Gm1 c00 c02 c03 Gh1 gc1 m11 m13 Gm2 c10 c11 c13 Gh2 Gc2 m21 m20 m23 c20 c21 c22 c23 "
       "r20 r21 r22 r23 yh").split(),
    t="M00 M01 M02 M03 C00 C01 C02 C03 M10 M11 M12 M13 C10 C11 C12 C13 M20 M21 M22 M23 C20 C21 C22 C23 H L".split(),
)


def rank_program(g, core, T, topo):
    rank = T.rank_of(core)
    if rank is None:
        return
    first, last = rank == 0, rank == len(T.cores) - 1
    eng = {"v": g.vector, "s": g.scalar, "t": g.tensor, "g": g, "y": g.sync}
    done = {"v": 0, "s": 0, "t": 0, "g": 0}
    known = {q: {} for q in eng}
    past = {}
    cut = CFG["cut"]

    def cover(a, b):
        return a != b and past.get(a, {}).get(b[0], 0) >= b[1]

    def need(q, deps):
        best = {}
        for s, n in deps:
            best[s] = max(n, best.get(s, 0))
        todo = [(s, n) for s, n in best.items() if known[q].get(s, 0) < n]
        todo = [d for d in todo if not any(cover(e, d) for e in todo)]
        for s, n in todo:
            eng[q].wait_ge(T.sem[s], n)
            for a, b in list(past.get((s, n), {}).items()) + [(s, n)]:
                known[q][a] = max(b, known[q].get(a, 0))

    def do(q, deps, call):
        need(q, deps)
        ins = call(eng[q])
        done[q] += 1
        s = "q" + q
        ins.then_inc(T.sem[s], 1)
        past[(s, done[q])] = dict(known[q])
        past[(s, done[q])][s] = done[q]
        return (s, done[q])

    def dma(q, sem, deps, out, in_):
        need(q, deps)
        eng[q].dma_start(out, in_).then_inc(T.sem[sem], 16)
        past[(sem, 16)] = dict(known[q])
        return (sem, 16)

    k = {}
    runs = lambda ends: list(zip(ends[:-1], ends[1:]))

    def load_w(a, b, deps):
        t = dma("y", "w%d" % a, deps, T.wb[:, 512 * a:512 * b], T.w[:, 512 * a:512 * b])
        for i in range(a, b):
            k["ld%d" % i] = [t]

    k["sf"] = [dma("y", "sf", [], T.sft[:], T.sf[:])]
    xc = 4 * CFG["xcut"]
    k["xh"] = [dma(CFG["qx"], "xh", [], T.xu[:, 128 + xc:1152], T.x[:, xc:1024])]
    k["xl"] = [dma("y", "xl", [], T.xu[:, 128:128 + xc], T.x[:, 0:xc])]
    for a, b in runs(CFG["wl"])[:CFG["early"]]:
        load_w(a, b, [])

    table = [(PLAIN, 48, 128, 16), (FIRST, 24, 16, 16),
             (HALO, 8, 128, 16), (HALO + 8, 1, 512, 0), (HALO + 9, 9, 256, 16)]
    i1 = do("g", [], lambda e: e.iota(T.part[:, 0:1], [[0, 1]], 0, 1))
    tab = [do("g", [], lambda e: e.iota(T.tab[:, a:a + n], [[s, n]], b, 0)) for a, n, b, s in table]
    k["tab1"], k["tab2"], k["tab"] = tab[1:2], tab[2:3], tab[-1:]

    def zero(buf, a, b):
        return do("g", [], lambda e: e.iota(buf[:, a:b], [[0, b - a]], 0, 0, allow_small_or_imprecise_dtypes=True))
    k["pad"] = [zero(T.g1, 272, 288), zero(T.u3, 384, 512)][-1:]
    do("v", [], lambda e: e.memset(T.xu[:, 1152:1280], 0.0))
    do("v", [], lambda e: e.memset(T.g0[:, 1440:1696], 0.0))
    low = do("v", [i1], lambda e: e.tensor_scalar(T.part[:, 1:2], T.part[:, 0:1], 15, None, AluOpType.bitwise_and))
    do("v", [], lambda e: e.memset(T.xu[:, 0:128], 0.0))
    k["zeros"] = [do("v", [low, tab[0]], lambda e: e.tensor_scalar(
        T.tabq[:], T.tab[:, PLAIN:FIRST], T.part[:, 1:2], 0.25, AluOpType.add, AluOpType.mult))]

    def list0(q, d):
        return [do(q, d, lambda e: e.tensor_scalar(
            T.off[:, PLAIN:FIRST], T.tabq[:], T.sft[:, 0:1], 4.0, AluOpType.subtract, AluOpType.mult))]

    def base(q, d):
        return [do(q, d, lambda e: e.tensor_scalar(T.base[:], T.sft[:], -4.0, T.part[:, 1:2], AluOpType.mult, AluOpType.add))]

    Q, S, G = [T.q0, T.q1, T.q2], [T.s0, T.s1, T.s2], [T.g0, T.g1, T.g2]
    U = [T.xu, T.z1, T.z2, T.z3]
    own = [32, 104, 72, 32]
    at = [104, 72, 32]
    Copy, Relu = ActivationFunctionType.Copy, ActivationFunctionType.Relu

    def lists(q, d, l, a, b, frm, bound, op):
        return [do(q, d, lambda e: e.tensor_scalar(
            T.off[:, 128 * l + a:128 * l + b], T.tab[:, frm:frm + b - a], T.base[:, l:l + 1], bound, AluOpType.add, op))]

    def pick(q, d, l, a, n, w0, w1, lst):
        if n == 0:
            return []
        out = G[l][:, 4 * a:4 * (a + n)]
        win = U[l][:, 4 * w0:4 * w1].indirect(T.off[:, 128 * l + lst:128 * l + lst + n // 4])
        if q == "s":
            return [do(q, d, lambda e: e.activation(out, win, Copy, scale=C if l else 1.0))]
        if l == 0:
            return [do(q, d, lambda e: e.tensor_copy(out, win))]
        return [do(q, d, lambda e: e.tensor_scalar(out, win, C, None, AluOpType.mult))]

    def gather(q, d, l, j0, j1):
        if l and j0 == 0:
            return pick(q, d, l, at[l], j1, own[l] - 4, own[l] + j1, FIRST)
        return pick(q, d, l, at[l] + j0, j1 - j0, own[l] + j0 - SH, own[l] + j1, PLAIN)

    def quant(q, d, codes, plane, tile, a, b):
        o = LATE if plane is T.s0 else 0
        return [do(q, d, lambda e: e.quantize_mx(codes[:, a:b], plane[:, o + a:o + b], tile[:, 4 * a:4 * b]))]

    def product(q, d, ps, l, i, a, n):
        c, o = 512 * l + 128 * i, a + (LATE if l == 0 else 0)
        return [do(q, d, lambda e: e.matmul_mx(
            ps[:, 512 * i:512 * i + n], T.qw[:, c:c + 128], T.sw[:, c:c + 128], Q[l][:, a:a + n], S[l][:, o:o + n], True, True))]

    def empty(q, d, src, out, scale):
        if q == "s":
            return [do(q, d, lambda e: e.activation(out, src, Relu, scale=C if scale else 1.0))]
        if scale:
            return [do(q, d, lambda e: e.tensor_scalar(out, src, 0.0, C, AluOpType.max, AluOpType.mult))]
        return [do(q, d, lambda e: e.tensor_scalar(out, src, 0.0, None, AluOpType.max))]

    def add(q, d, p, f):
        return [do(q, d, lambda e: e.tensor_tensor(p, p, f, AluOpType.add))]

    def scale(q, d, out, src):
        if q == "s":
            return [do(q, d, lambda e: e.activation(out, src, Copy, scale=C))]
        return [do(q, d, lambda e: e.tensor_scalar(out, src, C, None, AluOpType.mult))]

    def last_mm(q, d, ps, codes, plane, n):
        return [do(q, d, lambda e: e.matmul_mx(ps[:, 0:n], T.qv[:], T.sv[:], codes[:, 0:n], plane[:, 0:n], True, True))]

    def quant_high(q, d):
        return [do(q, d, lambda e: e.quantize_mx(T.q4[:], T.s4[:], T.u3[:, 512:1152]))]

    def store(q, d, ps, a, b, sem):
        if q == "s":
            t = do(q, d, lambda e: e.activation(T.yt[:, a:b], ps[:, 0:b - a], Copy))
        else:
            t = do(q, d, lambda e: e.tensor_copy(T.yt[:, a:b], ps[:, 0:b - a]))
        return [dma("y", sem, [t], T.y[:, a:b], T.yt[:, a:b])]

    nc, ns = int(CFG["msg"][0], 17), int(CFG["msg"][1], 17)

    def send(q, d):
        if CFG["halves"]:
            qa = [] if last else [do(q, d, lambda e: e.quantize_mx(T.qs[:], T.ss[:], T.g0[:, 1184:1696]))]
            codes, plane = T.qs[:, 0:104], T.ss[:, 0:104]
        else:
            qa = quant(q, d, T.q0, T.s0, T.g0, 296, 424)
            codes, plane = T.q0[:, 296:400], T.s0[:, LATE + 296:LATE + 400]
        if not last:
            dst = T.cores[rank + 1]
            rid, pid = topo.addr(dst)[0], topo.addr(dst)[1]
            use = topo.engines(core, dst)
            need("g", qa)
            g.remote_dma(T.q0[:, 0:104].bitcast(dt.uint8), codes.bitcast(dt.uint8), T.sem.rcv, T.sem.snt, pid, rid,
                         sum(1 << e for e in use[:nc]))
            g.remote_dma(T.s0[:, LATE:LATE + 104], plane, T.sem.rcv, T.sem.snt, pid, rid, sum(1 << e for e in use[-ns:]))
            if "off" in " ".join(CFG["gates"]):
                g.sem_inc(T.sem.off, 1)
        k.update(qa=qa, none=[], off=qa if last else [("off", 1)], snt=qa if last else [("snt", nc + ns)])
        late = runs(CFG["wl"])[CFG["early"]:] + [None]
        for j, r in enumerate(late):
            gate = [t for n in CFG["gates"][min(j, len(CFG["gates"]) - 1)].split("+") for t in k[n]]
            if r:
                load_w(r[0], r[1], gate)
            else:
                k["v"] = [dma("y", "v", gate, T.vb[:], T.v[:])]
        if first:
            k["nil"] = [zero(T.z1, 400, 416), zero(T.g1, 0, 272), zero(T.g2, 0, 128)][-1:]
        return qa

    k["rcv"] = [] if first else [("rcv", nc + ns)]
    M = [["m%d%d" % (l, i) for i in range(4)] for l in range(3)]
    K = [["c%d%d" % (l, i) for i in range(4)] for l in range(3)]
    A = [["a%d%d" % (l, i) for i in range(4)] if str(l) in CFG["bank"] else ["add%d" % l] for l in range(3)]
    a = cut["a"]
    steps = {
        "l0": (["sf", "zeros"], list0),
        "ga": (["l0", "xh"], gather, 0, 192, a), "Gy": (["l0", "xh"], gather, 0, a, 256),
        "Ga": (["l0", "xh"], pick, 0, at[0] + 260, 32, 256, 320, PLAIN),
        "gb": (["l0", "xl"], gather, 0, 0, cut["b"]), "Gb": (["l0", "xl", "xh"], gather, 0, cut["b"], 192),
        "qa": (["ga", "Ga", "Gy"], send),
        "qb": (["gb", "Gb"], quant, T.q0, T.s0, T.g0, 104, 296),
        "f1": (["base", "tab"], lists, 1, HALO, END, HALO, 256.0, AluOpType.min),
        "f2": (["base", "tab2"], lists, 2, HALO, HALO + 8, HALO, 128.0, AluOpType.min),
        "Gh1": (K[0] + ["f1"], pick, 1, 0, 68, 0, 68, HALO), "Gh2": (K[1] + ["f2"], pick, 2, 0, 32, 0, 36, HALO),
        "qv": (["v"], quant, T.qv, T.sv, T.vb, 0, 128),
        "sc": (A[2], scale, T.u3[:, 0:128], T.z3[:, 128:256]), "rest": (K[2], scale, T.u3[:, 128:384], T.z3[:, 256:512]),
        "all": (A[2], scale, T.u3[:, 0:384], T.z3[:, 128:512]),
        "qh": (M[2], quant_high),
        "ql": (["pad", "sc", "rest"], quant, T.q3, T.s3, T.u3, 0, 128),
        "base": (["zeros", "sf"], base),
        "H": (["qh", "qv"], last_mm, T.pm, T.q4, T.s4, 160), "L": (["ql", "qv"], last_mm, T.pc, T.q3, T.s3, 128),
        "yh": (["H"], store, T.pm, 96, 256, "yh"), "yl": (["L"], store, T.pc, 0, 96, "yl"),
    }
    W = {}
    for a, b in runs(CFG["wq"]):
        steps["w%d" % a] = (["ld%d" % i for i in range(a, b)], quant, T.qw, T.sw, T.wb, 128 * a, 128 * b)
        W.update({i: "w%d" % a for i in range(a, b)})
    for l in range(3):
        z, o, p = U[l + 1], 4 * own[l + 1], 32 * (l + 1)
        f, n = o - (128 if l == 2 else 144), at[l] + p
        steps["add%d" % l] = (K[l], add, z[:, o:o + 128], z[:, f:f + 128])
        for i in range(4):
            u, c = (T.u3, 512) if l == 2 else (z, o + 4 * p)
            steps["a%d%d" % (l, i)] = ([K[l][i]], add, z[:, o + i:o + 128:4], z[:, f + i:f + 128:4])
            steps["M%d%d" % (l, i)] = ((["qm%d" % l] if l else ["qa", "qb"]) + [W[4 * l + i]], product, T.pm, l, i, n, 256 - p)
            steps["C%d%d" % (l, i)] = ((["qc%d" % l] if l else ["qb", "rcv"]) + [W[4 * l + i]], product, T.pc, l, i, 0, n)
            steps[M[l][i]] = (["M%d%d" % (l, i)], empty, T.pm[:, 512 * i:512 * i + 256 - p], u[:, c + i:c + 4 * (256 - p):4], l == 2)
            steps[K[l][i]] = (["C%d%d" % (l, i)], empty, T.pc[:, 512 * i:512 * i + n], z[:, i:4 * n:4], False)
        if l:
            a, b, d = cut["m%d" % l], cut["c%d" % l], M[l - 1] + ["l%d" % l]
            steps["l%d" % l] = (["base", "tab1"], lists, l, PLAIN, HALO, PLAIN, 0.0, AluOpType.max)
            steps["gm%d" % l] = (d, gather, l, p, a)
            steps["Gm%d" % l] = (d, gather, l, a, 256)
            steps["gc%d" % l] = (d + A[l - 1], gather, l, 0, b)
            steps["Gc%d" % l] = (d + A[l - 1], gather, l, b, p)
            steps["qm%d" % l] = (["gm%d" % l, "Gm%d" % l], quant, Q[l], S[l], G[l], n, at[l] + 256)
            steps["qc%d" % l] = (["gc%d" % l, "Gc%d" % l, "Gh%d" % l, "pad"], quant, Q[l], S[l], G[l], 0, n)
    if cut["c2"] >= 64:
        steps["Gc2"] = (M[1] + K[1] + ["l2"],) + steps["Gc2"][1:]
    if "r20" in CFG["v"] + CFG["s"]:
        for i in range(4):
            steps[K[2][i]] = (["C2%d" % i], empty, T.pc[:, 512 * i:512 * i + 64], T.z3[:, i:256:4], False)
            steps["r2%d" % i] = ([K[2][i]], empty, T.pc[:, 512 * i + 64:512 * i + 128], T.u3[:, 128 + i:384:4], True)
        steps["ql"] = (["pad", "sc", "r20", "r21", "r22", "r23"],) + steps["ql"][1:]
    if CFG["halves"]:
        steps["Gx"] = (["l0", "xh"], gather, 0, 128, 192)
        steps["qx"] = (["ga", "Gy", "Gx"], quant, T.q0, T.s0, T.g0, 232, 360)
        steps["Gb"] = (["l0", "xl", "xh"], gather, 0, cut["b"], 128)
        steps["qb"] = (["gb", "Gb"], quant, T.q0, T.s0, T.g0, 104, 232)
        N = ["n0%d" % i for i in range(4)]
        for i in range(4):
            steps["A0%d" % i] = (["qx", W[i]], product, T.pc, 0, i, 232, 128)
            steps[N[i]] = (["A0%d" % i], empty, T.pc[:, 512 * i:512 * i + 128], T.z1[:, 928 + i:1440:4], False)
            steps["M0%d" % i] = (["qx", "qb", W[i]], product, T.pm, 0, i, 136, 128)
            steps[M[0][i]] = (["M0%d" % i], empty, T.pm[:, 512 * i:512 * i + 96], T.z1[:, 544 + i:928:4], False)
            steps["C0%d" % i] = (["qb", "rcv", N[i], W[i]],) + steps["C0%d" % i][1:]
        steps["gm1"] = (steps["gm1"][0] + N,) + steps["gm1"][1:]
        steps["Gm1"] = (N + ["l1"] + (M[0] if cut["m1"] < 160 else []),) + steps["Gm1"][1:]
    if first:
        for i in range(4):
            steps["C0%d" % i] = (steps["C0%d" % i][0], product, T.pc, 0, i, 104, 128)
            steps[K[0][i]] = (["C0%d" % i], empty, T.pc[:, 512 * i:512 * i + 32], T.z1[:, 416 + i:544:4], False)
        for n in ["f1", "f2", "Gh1", "Gh2"] + A[0] + A[1]:
            steps[n] = (steps[n][0] + ["nil"], lambda q, d: d)
    todo = {q: list(CFG[q]) for q in "vst"}
    while any(todo.values()):
        moved = False
        for q in todo:
            while todo[q] and all(d in k for d in steps[todo[q][0]][0]):
                n = todo[q].pop(0)
                k[n] = steps[n][1](q, [t for d in steps[n][0] for t in k[d]], *steps[n][2:])
                moved = True
        assert moved, todo
    need("g", ([] if last else [("snt", nc + ns)]) + [("q" + q, n) for q, n in done.items()] + k["yh"] + k["yl"])
